import numpy as np
import ml_dtypes


def mxq(x, axis, fmt="e4m3"):
    dtype, down = {"e4m3": (ml_dtypes.float8_e4m3fn, 7), "e5m2": (ml_dtypes.float8_e5m2, 14)}[fmt]
    v = np.moveaxis(np.asarray(x, np.float32).astype(ml_dtypes.bfloat16).astype(np.float64), axis, -1)
    blocks = v.reshape(v.shape[:-1] + (-1, 32))
    amax = np.abs(blocks).max(-1, keepdims=True)
    byte = np.maximum(np.where(amax > 0, np.frexp(amax)[1] - 1 + 127, 0) - down, 1)
    scale = np.exp2(byte - 127.0)
    codes = (blocks / scale).astype(np.float32).astype(dtype).astype(np.float64)
    return np.moveaxis((codes * scale).reshape(v.shape), -1, axis)


WIDE = False


def mx_kscale(k):
    if not WIDE:
        return np.ones(k)
    levels = np.array([10, -10, 5, -5, 0])
    if k % 512:
        return np.exp2(np.random.permutation(np.resize(levels, k // 32))).repeat(32)
    a = np.empty((k // 512, 16))
    for p in range(k // 512):
        a[p, :8] = np.random.permutation(np.resize(levels, 8))
        for g in range(8):
            far = levels[np.abs(levels - a[p, g]) >= 10]
            a[p, g + 8] = far[np.random.randint(len(far))]
    return np.exp2(a.ravel()).repeat(32)


def f64(x):
    return np.asarray(x).astype(np.float64)


def striped(idx):
    return np.tile(idx.reshape(-1, 16).T, (8, 1)).astype(np.uint16)


def unstriped(offs):
    return offs[:16].T.reshape(-1).astype(np.int64)


E2M1 = np.array([0.0, 0.5, 1.0, 1.5, 2.0, 3.0, 4.0, 6.0, -0.0, -0.5, -1.0, -1.5, -2.0, -3.0, -4.0, -6.0])


def pack_weight(w, fmt):
    k, n = w.shape
    w = f64(np.asarray(w, np.float32).astype(ml_dtypes.bfloat16)).reshape(k // 32, 32, n)
    amax = np.abs(w).max(1)
    if fmt == "e4m3":
        byte = np.frexp(amax)[1] - 1 + 127 - 7
    else:
        mant, ex = np.frexp(amax / 6.0)
        byte = np.where(mant > 0.5, ex, ex - 1) + 127
    byte = np.clip(np.where(amax > 0, byte, 1), 1, 254)
    scaled = (w * np.exp2(127.0 - byte)[:, None, :]).reshape(k, n).astype(np.float32)
    by_word = np.ascontiguousarray(scaled.reshape(k // 512, 128, 4, n).transpose(0, 1, 3, 2))
    if fmt == "e4m3":
        words = by_word.astype(ml_dtypes.float8_e4m3fn).view(np.uint8)
    else:
        c = by_word.astype(ml_dtypes.float4_e2m1fn).view(np.uint8) & 0xF
        words = (c[..., 0::2] | (c[..., 1::2] << 4)).reshape(k // 512, 128, 2 * n)
    return np.ascontiguousarray(words), np.ascontiguousarray(byte.astype(np.uint8).reshape(k // 512, 16, n))


def unpack_weight(words, scales, fmt):
    g, _, n = scales.shape
    words = np.ascontiguousarray(words).reshape(g, 128, n, -1)
    if fmt == "e4m3":
        vals = words.view(ml_dtypes.float8_e4m3fn).astype(np.float64)
    else:
        nib = np.empty((g, 128, n, 4), np.uint8)
        nib[..., 0::2] = words & 0xF
        nib[..., 1::2] = words >> 4
        vals = E2M1[nib]
    vals = vals * np.repeat(np.exp2(scales.astype(np.float64) - 127.0), 8, axis=1)[..., None]
    return vals.transpose(0, 1, 3, 2).reshape(g * 512, n)


def gelu(v):
    return 0.5 * v * (1.0 + np.tanh(np.sqrt(2.0 / np.pi) * (v + 0.044715 * v**3)))


K, H, T, S, T2, T3, S2, P = 1536, 1024, 2048, 512, 1024, 2048, 512, 512

def setup_inputs():
    n = np.random.standard_normal
    s = mx_kscale(K)[:, None]
    u = mx_kscale(H)[:, None]
    tab_words, tab_scales = pack_weight(n((K, T)) * s, "e4m3")
    tab2_words, tab2_scales = pack_weight(n((H, T3)) / np.sqrt(H) / u, "e4m3")
    w4_words, w4_scales = pack_weight(n((K, H)) / np.sqrt(K) / s * u.T, "e2m1")
    return {
        "tab_words": tab_words, "tab_scales": tab_scales,
        "offs": striped(np.random.permutation(T)[:S]),
        "w1": (2.0 * n((K, H)) / np.sqrt(K) / s).astype(np.float32),
        "b1": (0.7 * n(H)).astype(np.float32),
        "gain": (1.5 * np.exp(0.2 * n(H)) * u[:, 0]).astype(np.float32),
        "w4_words": w4_words, "w4_scales": w4_scales,
        "res": (n((H, S)) * u).astype(np.float32),
        "page0": (n((H, T2)) * u).astype(np.float32),
        "wgs": np.exp(0.3 * n((128, S))).astype(np.float32),
        "offs3": striped(np.random.permutation(T2)[:S]),
        "tab2_words": tab2_words, "tab2_scales": tab2_scales,
        "offs2": striped(np.random.permutation(T3)[:S2]),
        "pos1": striped(np.random.permutation(T2)[:P]),
        "pos2": striped(np.random.permutation(T2)[:P]),
        "rel": n((S2, P)).astype(np.float32),
    }

def reference(tab_words, tab_scales, offs, w1, b1, gain, w4_words, w4_scales, res, page0, wgs, offs3,
              tab2_words, tab2_scales, offs2, pos1, pos2, rel):
    v = unpack_weight(tab_words, tab_scales, "e4m3")[:, unstriped(offs)]
    w4 = unpack_weight(w4_words, w4_scales, "e2m1")
    bent = np.tanh((mxq(f64(w1), 0, "e4m3").T @ v) + f64(b1)[:, None])
    h = f64(gain)[:, None] * bent + (w4.T @ v)
    h = np.maximum(h, f64(res))
    page = f64(page0).copy()
    page[:, unstriped(offs3)] = np.tile(f64(wgs), (H // 128, 1)) * h
    v2 = unpack_weight(tab2_words, tab2_scales, "e4m3")[:, unstriped(offs2)]
    e = v2.T @ mxq(page, 0, "e4m3")
    return e[:, unstriped(pos1)] + e[:, unstriped(pos2)] * f64(rel)

@@ -1,0 +1,250 @@
+from contextlib import ExitStack
+
+import concourse.mybir as mybir
+from concourse.masks import make_identity
+
+K, H, T, S, T2, T3, S2, NP = 1536, 1024, 2048, 512, 1024, 2048, 512, 512
+FLOPS = 2 * (2 * K * H * S + H * S2 * T2)
+
+F32 = mybir.dt.float32
+BF16 = mybir.dt.bfloat16
+I32 = mybir.dt.int32
+U32 = mybir.dt.uint32
+U16 = mybir.dt.uint16
+U8 = mybir.dt.uint8
+FP8X4 = mybir.dt.float8_e4m3fn_x4
+FP4X4 = mybir.dt.float4_e2m1fn_x4
+MULT = mybir.AluOpType.mult
+ADD = mybir.AluOpType.add
+MAX = mybir.AluOpType.max
+TANH = mybir.ActivationFunctionType.Tanh
+
+P = 128
+KA = K // 512
+HA = H // 512
+TILES = H // P
+BANK = 512
+W1_CHUNKS = [(0, 1), (1, 1), (2, 2), (4, 2), (6, 2)]
+W4_FIRST = 2
+
+
+def tile_list_conodont_zone_scores_kernel(
+    tc, tab_words, tab_scales, offs, w1, b1, gain, w4_words, w4_scales, res, page0, wgs, offs3,
+    tab2_words, tab2_scales, offs2, pos1, pos2, rel, out,
+):
+    nc = tc.nc
+    with ExitStack() as ctx:
+        keep = ctx.enter_context(tc.tile_pool(name="keep", bufs=1))
+        ring2 = ctx.enter_context(tc.tile_pool(name="ring2", bufs=2))
+        ring3 = ctx.enter_context(tc.tile_pool(name="ring3", bufs=3))
+        psum = ctx.enter_context(tc.psum_pool(name="psum", bufs=2))
+
+        def load_list(src, name):
+            t = keep.tile([P, 32], U16, name=name)
+            nc.sync.dma_start(t[:], src)
+            return t
+
+        def load_words(src, a, name):
+            t = keep.tile([P, T], I32, name=name, align_bytes=64)
+            nc.sync.dma_start(t[:], src[a].rearrange("p t i -> p (t i)").bitcast(I32))
+            return t
+
+        tab_sc = keep.tile([P, KA, T], U8, name="tab_sc", align_bytes=64)
+        w4_sc = keep.tile([P, KA, H], U8, name="w4_sc", align_bytes=64)
+        tab2_sc = keep.tile([P, T3], U8, name="tab2_sc", align_bytes=64)
+        rows = keep.tile([P, P], F32, name="rows")
+        ident = keep.tile([P, P], F32, name="ident")
+        nc.vector.memset(w4_sc[:].rearrange("p a t -> p (a t)").bitcast(I32), 0)
+        nc.vector.memset(tab_sc[:].rearrange("p a t -> p (a t)").bitcast(I32), 0)
+        nc.vector.memset(rows[:], 0.0)
+        nc.vector.memset(tab2_sc[:].bitcast(I32), 0)
+        make_identity(nc, ident[:])
+        for q in range(4):
+            nc.gpsimd.dma_start(
+                w4_sc[32 * q : 32 * q + 4, :, :].bitcast(I32),
+                w4_scales[:, 4 * q : 4 * q + 4, :].rearrange("a r t -> r a t").bitcast(I32),
+            )
+
+        idx = load_list(offs, "idx")
+        idx3 = load_list(offs3, "idx3")
+        idx2 = load_list(offs2, "idx2")
+        p2 = load_list(pos2, "p2")
+        p1 = load_list(pos1, "p1")
+        tabw = [load_words(tab_words, a, f"tabw{a}") for a in range(KA)]
+        for q in range(4):
+            nc.sync.dma_start(
+                tab_sc[32 * q : 32 * q + 4, :, :].bitcast(I32),
+                tab_scales[:, 4 * q : 4 * q + 4, :].rearrange("a r t -> r a t").bitcast(I32),
+            )
+        nc.sync.dma_start(rows[0:TILES, :], b1.rearrange("(c p) -> c p", p=P))
+
+        w1_raw = {}
+        res_t = {}
+        page_t = {}
+
+        def load_w1(c0, n):
+            t = ring2.tile([P, KA, 4, n * P], F32, name="w1raw", tag="w1raw")
+            for a in range(KA):
+                nc.sync.dma_start(
+                    t[:, a, :, :],
+                    w1[512 * a : 512 * (a + 1), c0 * P : (c0 + n) * P].rearrange("(p j) c -> p j c", j=4),
+                )
+            for i in range(n):
+                w1_raw[c0 + i] = (t, i)
+
+        def load_w4(c0, c1, name):
+            t = keep.tile([P, KA, 2 * P * (c1 - c0)], U8, name=name, align_bytes=64)
+            nc.sync.dma_start(
+                t[:].bitcast(I32),
+                w4_words[:, :, 2 * P * c0 : 2 * P * c1].rearrange("a p b -> p a b").bitcast(I32),
+            )
+            return t
+
+        def load_res(c):
+            t = keep.tile([P, S], F32, name=f"res{c}")
+            nc.sync.dma_start(t[:], res[c * P : (c + 1) * P, :])
+            res_t[c] = t
+
+        def load_page(c):
+            t = keep.tile([P, T2], F32, name=f"page{c}")
+            nc.sync.dma_start(t[:], page0[c * P : (c + 1) * P, :])
+            page_t[c] = t
+
+        load_w1(*W1_CHUNKS[0])
+        nc.sync.dma_start(rows[TILES : 2 * TILES, :], gain.rearrange("(c p) -> c p", p=P))
+        w4_a = load_w4(0, W4_FIRST, "w4a")
+        load_res(0)
+        wgs_t = keep.tile([P, S], F32, name="wgs_t")
+        nc.sync.dma_start(wgs_t[:], wgs)
+        load_page(0)
+        w4_b = None
+        for c0, n in W1_CHUNKS[1:]:
+            load_w1(c0, n)
+            if c0 == W4_FIRST:
+                w4_b = load_w4(W4_FIRST, TILES, "w4b")
+            for c in range(c0, c0 + n):
+                load_res(c)
+                load_page(c)
+        for q in range(4):
+            nc.sync.dma_start(
+                tab2_sc[32 * q : 32 * q + 4 * HA, :].bitcast(I32),
+                tab2_scales[:, 4 * q : 4 * q + 4, :].bitcast(I32),
+            )
+        tab2w = [load_words(tab2_words, a, f"tab2w{a}") for a in range(HA)]
+        rel_t = []
+        for m in range(S2 // P):
+            t = keep.tile([P, NP], F32, name=f"rel{m}")
+            nc.sync.dma_start(t[:], rel[m * P : (m + 1) * P, :])
+            rel_t.append(t)
+
+        bg_ps = psum.tile([P, BANK], F32, name="bg_ps", tag="t1")
+        nc.tensor.transpose(bg_ps[:, 0:P], rows[:], ident[:])
+        bg = keep.tile([P, 2 * TILES], F32, name="bg")
+        nc.vector.tensor_copy(bg[:], bg_ps[:, 0 : 2 * TILES])
+
+        v_w = keep.tile([P, KA, S], I32, name="v_w", align_bytes=64)
+        v_s = keep.tile([P, KA, S], U8, name="v_s", align_bytes=64)
+        for a in range(KA):
+            nc.vector.tensor_copy(v_w[:, a, :].bitcast(U32), tabw[a][:].bitcast(U32).indirect(idx[:]))
+            nc.vector.tensor_copy(v_s[:, a, :], tab_sc[:, a, :].indirect(idx[:]))
+
+        page_w = keep.tile([P, HA, T2], I32, name="page_w", align_bytes=64)
+        page_s = keep.tile([P, HA, T2], U8, name="page_s", align_bytes=64)
+        turned = {}
+
+        for c in range(TILES):
+            raw, i = w1_raw[c]
+            grouped = ring3.tile([P, KA, P, 4], BF16, name="w1g", tag="w1g", align_bytes=64)
+            for a in range(KA):
+                nc.scalar.copy(
+                    grouped[:, a, :, :].rearrange("p (g i) j -> p g j i", i=4),
+                    raw[:, a, :, i * P : (i + 1) * P].rearrange("p j (g i) -> p g j i", i=4),
+                )
+            w1_w = ring3.tile([P, KA, P], I32, name="w1_w", tag="w1_w", align_bytes=64)
+            w1_s = ring3.tile([P, KA, P], U8, name="w1_s", tag="w1_s", align_bytes=64)
+            nc.vector.quantize_mx(
+                out=w1_w[:].rearrange("p a c -> p (a c)").bitcast(FP8X4),
+                scales=w1_s[:].rearrange("p a c -> p (a c)"),
+                in_=grouped[:].rearrange("p a c j -> p (a c j)"),
+            )
+            z = psum.tile([P, S], F32, name="z", tag="z")
+            y = psum.tile([P, S], F32, name="y", tag="y")
+            for a in range(KA):
+                nc.tensor.matmul_mx(
+                    out=z[:], lhsT=w1_w[:, a, :].bitcast(FP8X4), lhsT_scale=w1_s[:, a, :],
+                    rhs=v_w[:, a, :].bitcast(FP8X4), rhs_scale=v_s[:, a, :],
+                    start=(a == 0), stop=(a == KA - 1),
+                )
+            w4_t, ci = (w4_a, c) if c < W4_FIRST else (w4_b, c - W4_FIRST)
+            for a in range(KA):
+                nc.tensor.matmul_mx(
+                    out=y[:], lhsT=w4_t[:, a, 2 * P * ci : 2 * P * (ci + 1)].bitcast(FP4X4),
+                    lhsT_scale=w4_sc[:, a, c * P : (c + 1) * P],
+                    rhs=v_w[:, a, :].bitcast(FP8X4), rhs_scale=v_s[:, a, :],
+                    start=(a == 0), stop=(a == KA - 1),
+                )
+            bent = ring2.tile([P, S], F32, name="bent", tag="bent")
+            nc.scalar.activation(bent[:], z[:], TANH, bias=bg[:, c : c + 1])
+            summed = ring2.tile([P, S], F32, name="summed", tag="summed")
+            nc.vector.scalar_tensor_tensor(
+                summed[:], bent[:], bg[:, TILES + c : TILES + c + 1], y[:], MULT, ADD
+            )
+            h = ring2.tile([P, S], F32, name="h", tag="h")
+            nc.vector.tensor_tensor(h[:], summed[:], res_t[c][:], MAX)
+            nc.vector.tensor_tensor(page_t[c][:].indirect(idx3[:]), h[:], wgs_t[:], MULT)
+
+            a2, q = divmod(c, 4)
+            for half in range(2):
+                if q == 0:
+                    turned[a2, half] = keep.tile([P, 4, 2, 256], BF16, name=f"turned{a2}{half}", align_bytes=64)
+                t1 = psum.tile([P, 4, P], F32, name="t1", tag="t1")
+                for b in range(4):
+                    n0 = (4 * half + b) * P
+                    nc.tensor.transpose(t1[:, b, :], page_t[c][:, n0 : n0 + P], ident[:])
+                nc.scalar.copy(
+                    turned[a2, half][:, :, :, 64 * q : 64 * (q + 1)].rearrange("p b u (m e) -> p b u m e", e=2),
+                    t1[:].rearrange("p b (m u e) -> p b u m e", u=2, e=2),
+                )
+            if q == 3:
+                for half in range(2):
+                    words = turned[a2, half][:].bitcast(F32)
+                    pg = ring2.tile([P, 4 * BANK], BF16, name="pg", tag="pg", align_bytes=64)
+                    pg_words = pg[:].bitcast(F32).rearrange("p (b n u) -> p b n u", b=4, u=2)
+                    for pair in range(2):
+                        t2 = psum.tile([P, 2, 2, P], F32, name="t2", tag="t2")
+                        for b in range(2):
+                            for u in range(2):
+                                nc.tensor.transpose(t2[:, b, u, :], words[:, 2 * pair + b, u, :], ident[:])
+                        nc.scalar.copy(
+                            pg_words[:, 2 * pair : 2 * pair + 2, :, :], t2[:].rearrange("p b u n -> p b n u")
+                        )
+                    nc.vector.quantize_mx(
+                        out=page_w[:, a2, half * BANK : (half + 1) * BANK].bitcast(FP8X4),
+                        scales=page_s[:, a2, half * BANK : (half + 1) * BANK],
+                        in_=pg[:],
+                    )
+
+        v2_w = keep.tile([P, HA, S2], I32, name="v2_w", align_bytes=64)
+        v2_s = keep.tile([P, S2], U8, name="v2_s", align_bytes=64)
+        nc.vector.tensor_copy(v2_s[:], tab2_sc[:].indirect(idx2[:]))
+        for a in range(HA):
+            nc.vector.tensor_copy(v2_w[:, a, :].bitcast(U32), tab2w[a][:].bitcast(U32).indirect(idx2[:]))
+
+        for m in range(S2 // P):
+            e = ring2.tile([P, T2], F32, name="e", tag="e")
+            for half in range(2):
+                acc = psum.tile([P, BANK], F32, name="acc", tag="zy"[half])
+                for a in range(HA):
+                    nc.tensor.matmul_mx(
+                        out=acc[:], lhsT=v2_w[:, a, m * P : (m + 1) * P].bitcast(FP8X4),
+                        lhsT_scale=v2_s[4 * a : P, m * P : (m + 1) * P],
+                        rhs=page_w[:, a, half * BANK : (half + 1) * BANK].bitcast(FP8X4),
+                        rhs_scale=page_s[:, a, half * BANK : (half + 1) * BANK],
+                        start=(a == 0), stop=(a == HA - 1),
+                    )
+                nc.scalar.copy(e[:, half * BANK : (half + 1) * BANK], acc[:])
+            lower = ring2.tile([P, NP], F32, name="lower", tag="lower")
+            nc.vector.tensor_tensor(lower[:], e[:].indirect(p2[:]), rel_t[m][:], MULT)
+            both = ring2.tile([P, NP], F32, name="both", tag="both")
+            nc.vector.tensor_tensor(both[:], e[:].indirect(p1[:]), lower[:], ADD)
+            nc.sync.dma_start(out[m * P : (m + 1) * P, :], both[:])

@@ -24,8 +24,7 @@ KA = K // 512
 HA = H // 512
 TILES = H // P
 BANK = 512
-W1_CHUNKS = [(0, 1), (1, 1), (2, 2), (4, 2), (6, 2)]
-W4_FIRST = 2
+W4_PARTS = [(0, 2), (2, 4), (4, 8)]
 
 
 def tile_list_conodont_zone_scores_kernel(
@@ -36,8 +35,11 @@ def tile_list_conodont_zone_scores_kernel(
     with ExitStack() as ctx:
         keep = ctx.enter_context(tc.tile_pool(name="keep", bufs=1))
         ring2 = ctx.enter_context(tc.tile_pool(name="ring2", bufs=2))
-        ring3 = ctx.enter_context(tc.tile_pool(name="ring3", bufs=3))
+        ends = ctx.enter_context(tc.tile_pool(name="ends", bufs=1))
+        held = ctx.enter_context(tc.tile_pool(name="held", bufs=1))
+        late = ctx.enter_context(tc.tile_pool(name="late", bufs=1))
         psum = ctx.enter_context(tc.psum_pool(name="psum", bufs=2))
+        psum1 = ctx.enter_context(tc.psum_pool(name="psum1", bufs=1))
 
         def load_list(src, name):
             t = keep.tile([P, 32], U16, name=name)
@@ -50,58 +52,60 @@ def tile_list_conodont_zone_scores_kernel(
             return t
 
         tab_sc = keep.tile([P, KA, T], U8, name="tab_sc", align_bytes=64)
-        w4_sc = keep.tile([P, KA, H], U8, name="w4_sc", align_bytes=64)
+        w4_sc = [
+            keep.tile([P, KA, 2 * P], U8, name="w4_sc0", align_bytes=64),
+            keep.tile([P, KA, H - 2 * P], U8, name="w4_sc1", align_bytes=64),
+        ]
         tab2_sc = keep.tile([P, T3], U8, name="tab2_sc", align_bytes=64)
         rows = keep.tile([P, P], F32, name="rows")
         ident = keep.tile([P, P], F32, name="ident")
-        nc.vector.memset(w4_sc[:].rearrange("p a t -> p (a t)").bitcast(I32), 0)
         nc.vector.memset(tab_sc[:].rearrange("p a t -> p (a t)").bitcast(I32), 0)
-        nc.vector.memset(rows[:], 0.0)
+        for t in w4_sc:
+            nc.vector.memset(t[:].rearrange("p a t -> p (a t)").bitcast(I32), 0)
         nc.vector.memset(tab2_sc[:].bitcast(I32), 0)
+        nc.gpsimd.memset(rows[:], 0.0)
         make_identity(nc, ident[:])
-        for q in range(4):
-            nc.gpsimd.dma_start(
-                w4_sc[32 * q : 32 * q + 4, :, :].bitcast(I32),
-                w4_scales[:, 4 * q : 4 * q + 4, :].rearrange("a r t -> r a t").bitcast(I32),
-            )
 
         idx = load_list(offs, "idx")
         idx3 = load_list(offs3, "idx3")
         idx2 = load_list(offs2, "idx2")
         p2 = load_list(pos2, "p2")
         p1 = load_list(pos1, "p1")
-        tabw = [load_words(tab_words, a, f"tabw{a}") for a in range(KA)]
-        for q in range(4):
-            nc.sync.dma_start(
-                tab_sc[32 * q : 32 * q + 4, :, :].bitcast(I32),
-                tab_scales[:, 4 * q : 4 * q + 4, :].rearrange("a r t -> r a t").bitcast(I32),
-            )
-        nc.sync.dma_start(rows[0:TILES, :], b1.rearrange("(c p) -> c p", p=P))
 
         w1_raw = {}
+        w4_t = {}
         res_t = {}
         page_t = {}
 
-        def load_w1(c0, n):
-            t = ring2.tile([P, KA, 4, n * P], F32, name="w1raw", tag="w1raw")
-            for a in range(KA):
+        def load_w1(c0, passes):
+            if c0 not in w1_raw:
+                t = ring2.tile([P, KA, 4, 2 * P], F32, name="w1raw", tag="w1raw")
+                for i in range(2):
+                    w1_raw[c0 + i] = (t, i)
+            for a in passes:
                 nc.sync.dma_start(
-                    t[:, a, :, :],
-                    w1[512 * a : 512 * (a + 1), c0 * P : (c0 + n) * P].rearrange("(p j) c -> p j c", j=4),
+                    w1_raw[c0][0][:, a, :, :],
+                    w1[512 * a : 512 * (a + 1), c0 * P : (c0 + 2) * P].rearrange("(p j) c -> p j c", j=4),
                 )
-            for i in range(n):
-                w1_raw[c0 + i] = (t, i)
 
-        def load_w4(c0, c1, name):
-            t = keep.tile([P, KA, 2 * P * (c1 - c0)], U8, name=name, align_bytes=64)
+        def load_w4(c0, c1):
+            t = keep.tile([P, KA, 2 * P * (c1 - c0)], U8, name=f"w4_{c0}", align_bytes=64)
             nc.sync.dma_start(
                 t[:].bitcast(I32),
                 w4_words[:, :, 2 * P * c0 : 2 * P * c1].rearrange("a p b -> p a b").bitcast(I32),
             )
-            return t
+            for c in range(c0, c1):
+                w4_t[c] = (t, c - c0)
+
+        def load_w4_scales(t, r0, r1):
+            for q in range(4):
+                nc.sync.dma_start(
+                    t[32 * q : 32 * q + 4, :, :].bitcast(I32),
+                    w4_scales[:, 4 * q : 4 * q + 4, r0:r1].rearrange("a r t -> r a t").bitcast(I32),
+                )
 
         def load_res(c):
-            t = keep.tile([P, S], F32, name=f"res{c}")
+            t = keep.tile([P, S], F32, name=f"res{c}", tag=f"res{c}")
             nc.sync.dma_start(t[:], res[c * P : (c + 1) * P, :])
             res_t[c] = t
 
@@ -110,21 +114,34 @@ def tile_list_conodont_zone_scores_kernel(
             nc.sync.dma_start(t[:], page0[c * P : (c + 1) * P, :])
             page_t[c] = t
 
-        load_w1(*W1_CHUNKS[0])
+        tabw = [load_words(tab_words, 0, "tabw0")]
+        load_w4(*W4_PARTS[0])
+        load_w1(0, [0])
+        for q in range(4):
+            nc.sync.dma_start(
+                tab_sc[32 * q : 32 * q + 4, :, :].bitcast(I32),
+                tab_scales[:, 4 * q : 4 * q + 4, :].rearrange("a r t -> r a t").bitcast(I32),
+            )
+        for a in range(1, KA):
+            tabw.append(load_words(tab_words, a, f"tabw{a}"))
+        nc.sync.dma_start(rows[0:TILES, :], b1.rearrange("(c p) -> c p", p=P))
         nc.sync.dma_start(rows[TILES : 2 * TILES, :], gain.rearrange("(c p) -> c p", p=P))
-        w4_a = load_w4(0, W4_FIRST, "w4a")
-        load_res(0)
-        wgs_t = keep.tile([P, S], F32, name="wgs_t")
-        nc.sync.dma_start(wgs_t[:], wgs)
+        load_w4_scales(w4_sc[0], 0, 2 * P)
+        load_w1(0, range(1, KA))
         load_page(0)
-        w4_b = None
-        for c0, n in W1_CHUNKS[1:]:
-            load_w1(c0, n)
-            if c0 == W4_FIRST:
-                w4_b = load_w4(W4_FIRST, TILES, "w4b")
-            for c in range(c0, c0 + n):
-                load_res(c)
-                load_page(c)
+        wgs_t = late.tile([P, S], F32, name="wgs_t", offset=2048, align_bytes=64)
+        nc.sync.dma_start(wgs_t[:], wgs)
+        load_res(0)
+        load_w1(2, range(KA))
+        load_w4_scales(w4_sc[1], 2 * P, H)
+        load_w4(*W4_PARTS[1])
+        for c in range(1, TILES):
+            if c % 2 == 0 and c + 2 < TILES:
+                load_w1(c + 2, range(KA))
+            if c == 2:
+                load_w4(*W4_PARTS[2])
+            load_page(c)
+            load_res(c)
         for q in range(4):
             nc.sync.dma_start(
                 tab2_sc[32 * q : 32 * q + 4 * HA, :].bitcast(I32),
@@ -133,14 +150,23 @@ def tile_list_conodont_zone_scores_kernel(
         tab2w = [load_words(tab2_words, a, f"tab2w{a}") for a in range(HA)]
         rel_t = []
         for m in range(S2 // P):
-            t = keep.tile([P, NP], F32, name=f"rel{m}")
+            t = ends.tile([P, NP], F32, name=f"rel{m}", offset=4 * NP * m)
             nc.sync.dma_start(t[:], rel[m * P : (m + 1) * P, :])
             rel_t.append(t)
 
-        bg_ps = psum.tile([P, BANK], F32, name="bg_ps", tag="t1")
+        bg_ps = psum.tile([P, BANK], F32, name="bg_ps", tag="t2")
         nc.tensor.transpose(bg_ps[:, 0:P], rows[:], ident[:])
-        bg = keep.tile([P, 2 * TILES], F32, name="bg")
-        nc.vector.tensor_copy(bg[:], bg_ps[:, 0 : 2 * TILES])
+
+        def bias_at(c):
+            return ((c + 1) % 2) * 2432 + 2048 + 64 * ((c + 1) // 2)
+
+        bias = []
+        for c in range(TILES):
+            t = held.tile([P, 1], F32, name=f"bias{c}", offset=bias_at(c), align_bytes=64)
+            nc.scalar.copy(t[:], bg_ps[:, c : c + 1])
+            bias.append(t)
+        gains = keep.tile([P, TILES], F32, name="gains")
+        nc.scalar.copy(gains[:], bg_ps[:, TILES : 2 * TILES])
 
         v_w = keep.tile([P, KA, S], I32, name="v_w", align_bytes=64)
         v_s = keep.tile([P, KA, S], U8, name="v_s", align_bytes=64)
@@ -148,56 +174,85 @@ def tile_list_conodont_zone_scores_kernel(
             nc.vector.tensor_copy(v_w[:, a, :].bitcast(U32), tabw[a][:].bitcast(U32).indirect(idx[:]))
             nc.vector.tensor_copy(v_s[:, a, :], tab_sc[:, a, :].indirect(idx[:]))
 
-        page_w = keep.tile([P, HA, T2], I32, name="page_w", align_bytes=64)
-        page_s = keep.tile([P, HA, T2], U8, name="page_s", align_bytes=64)
+        grouped = {}
+        codes = {}
+        bent = {}
+        y_ps = {}
+        summed = {}
+        bounded = {}
         turned = {}
+        pg = {}
 
-        for c in range(TILES):
+        def round_w1(c):
             raw, i = w1_raw[c]
-            grouped = ring3.tile([P, KA, P, 4], BF16, name="w1g", tag="w1g", align_bytes=64)
+            g = ring2.tile([P, KA, P, 4], BF16, name="w1g", tag="w1g", align_bytes=64)
             for a in range(KA):
                 nc.scalar.copy(
-                    grouped[:, a, :, :].rearrange("p (g i) j -> p g j i", i=4),
+                    g[:, a, :, :].rearrange("p (g i) j -> p g j i", i=4),
                     raw[:, a, :, i * P : (i + 1) * P].rearrange("p j (g i) -> p g j i", i=4),
                 )
-            w1_w = ring3.tile([P, KA, P], I32, name="w1_w", tag="w1_w", align_bytes=64)
-            w1_s = ring3.tile([P, KA, P], U8, name="w1_s", tag="w1_s", align_bytes=64)
+            grouped[c] = g
+
+        def quantise_w1(c, a0, a1):
+            if a0 == 0:
+                w1_w = held.tile([P, KA, P], I32, name=f"w1_w{c}", offset=bias_at(c - 1) + 64 - 1536, align_bytes=64)
+                w1_s = ring2.tile([P, KA, P], U8, name="w1_s", tag="w1_s", align_bytes=64)
+                codes[c] = (w1_w, w1_s)
+            w1_w, w1_s = codes[c]
             nc.vector.quantize_mx(
-                out=w1_w[:].rearrange("p a c -> p (a c)").bitcast(FP8X4),
-                scales=w1_s[:].rearrange("p a c -> p (a c)"),
-                in_=grouped[:].rearrange("p a c j -> p (a c j)"),
+                out=w1_w[:, a0:a1, :].rearrange("p a c -> p (a c)").bitcast(FP8X4),
+                scales=w1_s[:, a0:a1, :].rearrange("p a c -> p (a c)"),
+                in_=grouped[c][:, a0:a1, :, :].rearrange("p a c j -> p (a c j)"),
             )
-            z = psum.tile([P, S], F32, name="z", tag="z")
-            y = psum.tile([P, S], F32, name="y", tag="y")
+
+        def product_w4(c):
+            y = psum1.tile([P, S], F32, name="y", tag=f"p{c % 2}")
+            w4, ci = w4_t[c]
+            sc, si = (w4_sc[0], c) if c < 2 else (w4_sc[1], c - 2)
+            for a in range(KA):
+                nc.tensor.matmul_mx(
+                    out=y[:], lhsT=w4[:, a, 2 * P * ci : 2 * P * (ci + 1)].bitcast(FP4X4),
+                    lhsT_scale=sc[:, a, si * P : (si + 1) * P],
+                    rhs=v_w[:, a, :].bitcast(FP8X4), rhs_scale=v_s[:, a, :],
+                    start=(a == 0), stop=(a == KA - 1),
+                )
+            y_ps[c] = y
+
+        def product_w1(c):
+            w1_w, w1_s = codes[c]
+            z = psum1.tile([P, S], F32, name="z", tag="z")
             for a in range(KA):
                 nc.tensor.matmul_mx(
                     out=z[:], lhsT=w1_w[:, a, :].bitcast(FP8X4), lhsT_scale=w1_s[:, a, :],
                     rhs=v_w[:, a, :].bitcast(FP8X4), rhs_scale=v_s[:, a, :],
                     start=(a == 0), stop=(a == KA - 1),
                 )
-            w4_t, ci = (w4_a, c) if c < W4_FIRST else (w4_b, c - W4_FIRST)
-            for a in range(KA):
-                nc.tensor.matmul_mx(
-                    out=y[:], lhsT=w4_t[:, a, 2 * P * ci : 2 * P * (ci + 1)].bitcast(FP4X4),
-                    lhsT_scale=w4_sc[:, a, c * P : (c + 1) * P],
-                    rhs=v_w[:, a, :].bitcast(FP8X4), rhs_scale=v_s[:, a, :],
-                    start=(a == 0), stop=(a == KA - 1),
-                )
-            bent = ring2.tile([P, S], F32, name="bent", tag="bent")
-            nc.scalar.activation(bent[:], z[:], TANH, bias=bg[:, c : c + 1])
-            summed = ring2.tile([P, S], F32, name="summed", tag="summed")
+            t = ring2.tile([P, S], F32, name="bent", tag="bent")
+            nc.scalar.activation(t[:], z[:], TANH, bias=bias[c][:])
+            bent[c] = t
+
+        def add_up(c):
+            t = keep.tile([P, S], F32, name="summed", tag="summed")
             nc.vector.scalar_tensor_tensor(
-                summed[:], bent[:], bg[:, TILES + c : TILES + c + 1], y[:], MULT, ADD
+                t[:], bent[c][:], gains[:, c : c + 1], y_ps[c][:], MULT, ADD
             )
-            h = ring2.tile([P, S], F32, name="h", tag="h")
-            nc.vector.tensor_tensor(h[:], summed[:], res_t[c][:], MAX)
+            summed[c] = t
+
+        def bound(c):
+            h = held.tile([P, S], F32, name=f"h{c}", offset=(c % 2) * 2432, align_bytes=64)
+            nc.vector.tensor_tensor(h[:], summed[c][:], res_t[c][:], MAX)
+            bounded[c] = h
+
+        def place(c):
+            h = bounded[c]
             nc.vector.tensor_tensor(page_t[c][:].indirect(idx3[:]), h[:], wgs_t[:], MULT)
 
+        def turn(c):
             a2, q = divmod(c, 4)
             for half in range(2):
+                t1 = psum1.tile([P, 4, P], F32, name="t1", tag="z" if c == 0 else ("t1", f"p{(c + 1) % 2}")[half])
                 if q == 0:
                     turned[a2, half] = keep.tile([P, 4, 2, 256], BF16, name=f"turned{a2}{half}", align_bytes=64)
-                t1 = psum.tile([P, 4, P], F32, name="t1", tag="t1")
                 for b in range(4):
                     n0 = (4 * half + b) * P
                     nc.tensor.transpose(t1[:, b, :], page_t[c][:, n0 : n0 + P], ident[:])
@@ -205,46 +260,104 @@ def tile_list_conodont_zone_scores_kernel(
                     turned[a2, half][:, :, :, 64 * q : 64 * (q + 1)].rearrange("p b u (m e) -> p b u m e", e=2),
                     t1[:].rearrange("p b (m u e) -> p b u m e", u=2, e=2),
                 )
-            if q == 3:
+
+        def turn_back(a2, half):
+            words = turned[a2, half][:].bitcast(F32)
+            g = keep.tile([P, 4 * BANK], BF16, name="pg", tag=f"pg{a2}{half}", align_bytes=64)
+            g_words = g[:].bitcast(F32).rearrange("p (b n u) -> p b n u", b=4, u=2)
+            for pair in range(2):
+                if a2 == 0:
+                    t2 = psum1.tile([P, 2, 2, P], F32, name="t2", tag=("p0", "z")[pair])
+                else:
+                    t2 = psum.tile([P, 2, 2, P], F32, name="t2", tag="t2")
+                for b in range(2):
+                    for u in range(2):
+                        nc.tensor.transpose(t2[:, b, u, :], words[:, 2 * pair + b, u, :], ident[:])
+                nc.scalar.copy(g_words[:, 2 * pair : 2 * pair + 2, :, :], t2[:].rearrange("p b u n -> p b n u"))
+            pg[a2, half] = g
+
+        round_w1(0)
+        round_w1(1)
+        quantise_w1(0, 0, 2)
+        quantise_w1(0, 2, 3)
+        product_w4(0)
+        product_w1(0)
+        product_w4(1)
+        for c in range(TILES):
+            add_up(c)
+            if c + 1 < TILES:
+                quantise_w1(c + 1, 0, 2)
+            bound(c)
+            if c + 1 < TILES:
+                quantise_w1(c + 1, 2, 3)
+            place(c)
+            if c + 2 < TILES:
+                round_w1(c + 2)
+            if c + 1 < TILES:
+                product_w1(c + 1)
+            if c >= 1:
+                turn(c - 1)
+            if c + 2 < TILES:
+                product_w4(c + 2)
+            if c == TILES - 2:
                 for half in range(2):
-                    words = turned[a2, half][:].bitcast(F32)
-                    pg = ring2.tile([P, 4 * BANK], BF16, name="pg", tag="pg", align_bytes=64)
-                    pg_words = pg[:].bitcast(F32).rearrange("p (b n u) -> p b n u", b=4, u=2)
-                    for pair in range(2):
-                        t2 = psum.tile([P, 2, 2, P], F32, name="t2", tag="t2")
-                        for b in range(2):
-                            for u in range(2):
-                                nc.tensor.transpose(t2[:, b, u, :], words[:, 2 * pair + b, u, :], ident[:])
-                        nc.scalar.copy(
-                            pg_words[:, 2 * pair : 2 * pair + 2, :, :], t2[:].rearrange("p b u n -> p b n u")
-                        )
-                    nc.vector.quantize_mx(
-                        out=page_w[:, a2, half * BANK : (half + 1) * BANK].bitcast(FP8X4),
-                        scales=page_s[:, a2, half * BANK : (half + 1) * BANK],
-                        in_=pg[:],
-                    )
+                    turn_back(0, half)
+        turn(TILES - 1)
+        for half in range(2):
+            turn_back(1, half)
 
-        v2_w = keep.tile([P, HA, S2], I32, name="v2_w", align_bytes=64)
-        v2_s = keep.tile([P, S2], U8, name="v2_s", align_bytes=64)
+        v2_s = late.tile([P, S2], U8, name="v2_s", offset=2560, align_bytes=64)
+        page_s = late.tile([P, HA, T2], U8, name="page_s", offset=512, align_bytes=64)
+        page_w = keep.tile([P, HA, T2], I32, name="page_w", align_bytes=64)
+        v2_w = []
+
+        def gather_v2(t, part):
+            for a in range(HA):
+                nc.vector.tensor_copy(
+                    t[:, a, :].bitcast(U32), tab2w[a][:].bitcast(U32).indirect(idx2[:, 16 * part : 16 * (part + 1)])
+                )
+            v2_w.append(t)
+
         nc.vector.tensor_copy(v2_s[:], tab2_sc[:].indirect(idx2[:]))
+        gather_v2(late.tile([P, HA, S2 // 2], I32, name="v2_lo", offset=3072, align_bytes=64), 0)
         for a in range(HA):
-            nc.vector.tensor_copy(v2_w[:, a, :].bitcast(U32), tab2w[a][:].bitcast(U32).indirect(idx2[:]))
-
-        for m in range(S2 // P):
-            e = ring2.tile([P, T2], F32, name="e", tag="e")
             for half in range(2):
-                acc = psum.tile([P, BANK], F32, name="acc", tag="zy"[half])
-                for a in range(HA):
+                nc.vector.quantize_mx(
+                    out=page_w[:, a, half * BANK : (half + 1) * BANK].bitcast(FP8X4),
+                    scales=page_s[:, a, half * BANK : (half + 1) * BANK],
+                    in_=pg[a, half][:],
+                )
+        gather_v2(keep.tile([P, HA, S2 // 2], I32, name="v2_hi", tag="pg11", align_bytes=64), 1)
+
+        scores = {}
+        lower = {}
+        for m in range(S2 // P):
+            e = keep.tile([P, T2], F32, name=f"e{m}")
+            for half in range(2):
+                if m % 2 == 0:
+                    acc = psum.tile([P, BANK], F32, name="acc", tag="t2")
+                else:
+                    acc = psum1.tile([P, BANK], F32, name="acc", tag=("z", "p1")[half])
+                order = range(HA) if m == 0 else reversed(range(HA))
+                for i, a in enumerate(order):
                     nc.tensor.matmul_mx(
-                        out=acc[:], lhsT=v2_w[:, a, m * P : (m + 1) * P].bitcast(FP8X4),
+                        out=acc[:], lhsT=v2_w[m // 2][:, a, (m % 2) * P : (m % 2 + 1) * P].bitcast(FP8X4),
                         lhsT_scale=v2_s[4 * a : P, m * P : (m + 1) * P],
                         rhs=page_w[:, a, half * BANK : (half + 1) * BANK].bitcast(FP8X4),
                         rhs_scale=page_s[:, a, half * BANK : (half + 1) * BANK],
-                        start=(a == 0), stop=(a == HA - 1),
+                        start=(i == 0), stop=(i == HA - 1),
                     )
                 nc.scalar.copy(e[:, half * BANK : (half + 1) * BANK], acc[:])
-            lower = ring2.tile([P, NP], F32, name="lower", tag="lower")
-            nc.vector.tensor_tensor(lower[:], e[:].indirect(p2[:]), rel_t[m][:], MULT)
-            both = ring2.tile([P, NP], F32, name="both", tag="both")
-            nc.vector.tensor_tensor(both[:], e[:].indirect(p1[:]), lower[:], ADD)
-            nc.sync.dma_start(out[m * P : (m + 1) * P, :], both[:])
+            scores[m] = e
+            t = keep.tile([P, NP], F32, name="lower", tag=f"res{m}")
+            nc.vector.tensor_tensor(t[:], e[:].indirect(p2[:]), rel_t[m][:], MULT)
+            lower[m] = t
+        both = ends.tile([P, S2 // P, NP], F32, name="both", offset=0)
+        for m in range(S2 // P):
+            pieces = 2 if m == S2 // P - 1 else 1
+            width = NP // pieces
+            for j0 in range(0, NP, width):
+                cols = slice(j0, j0 + width)
+                picked = scores[m][:].indirect(p1[:, j0 // 16 : (j0 + width) // 16])
+                nc.vector.tensor_tensor(both[:, m, cols], picked, lower[m][:, cols], ADD)
+                nc.sync.dma_start(out[m * P : (m + 1) * P, cols], both[:, m, cols])

from contextlib import ExitStack

import concourse.mybir as mybir
from concourse.masks import make_identity

K, H, T, S, T2, T3, S2, NP = 1536, 1024, 2048, 512, 1024, 2048, 512, 512
FLOPS = 2 * (2 * K * H * S + H * S2 * T2)

F32 = mybir.dt.float32
BF16 = mybir.dt.bfloat16
I32 = mybir.dt.int32
U32 = mybir.dt.uint32
U16 = mybir.dt.uint16
U8 = mybir.dt.uint8
FP8X4 = mybir.dt.float8_e4m3fn_x4
FP4X4 = mybir.dt.float4_e2m1fn_x4
MULT = mybir.AluOpType.mult
ADD = mybir.AluOpType.add
MAX = mybir.AluOpType.max
TANH = mybir.ActivationFunctionType.Tanh

P = 128
KA = K // 512
HA = H // 512
TILES = H // P
BANK = 512
W4_PARTS = [(0, 2), (2, 4), (4, 8)]


def tile_list_conodont_zone_scores_kernel(
    tc, tab_words, tab_scales, offs, w1, b1, gain, w4_words, w4_scales, res, page0, wgs, offs3,
    tab2_words, tab2_scales, offs2, pos1, pos2, rel, out,
):
    nc = tc.nc
    with ExitStack() as ctx:
        keep = ctx.enter_context(tc.tile_pool(name="keep", bufs=1))
        ring2 = ctx.enter_context(tc.tile_pool(name="ring2", bufs=2))
        ends = ctx.enter_context(tc.tile_pool(name="ends", bufs=1))
        held = ctx.enter_context(tc.tile_pool(name="held", bufs=1))
        late = ctx.enter_context(tc.tile_pool(name="late", bufs=1))
        psum = ctx.enter_context(tc.psum_pool(name="psum", bufs=2))
        psum1 = ctx.enter_context(tc.psum_pool(name="psum1", bufs=1))

        def load_list(src, name):
            t = keep.tile([P, 32], U16, name=name)
            nc.sync.dma_start(t[:], src)
            return t

        def load_words(src, a, name):
            t = keep.tile([P, T], I32, name=name, align_bytes=64)
            nc.sync.dma_start(t[:], src[a].rearrange("p t i -> p (t i)").bitcast(I32))
            return t

        tab_sc = keep.tile([P, KA, T], U8, name="tab_sc", align_bytes=64)
        w4_sc = [
            keep.tile([P, KA, 2 * P], U8, name="w4_sc0", align_bytes=64),
            keep.tile([P, KA, H - 2 * P], U8, name="w4_sc1", align_bytes=64),
        ]
        tab2_sc = keep.tile([P, T3], U8, name="tab2_sc", align_bytes=64)
        rows = keep.tile([P, P], F32, name="rows")
        ident = keep.tile([P, P], F32, name="ident")
        nc.vector.memset(tab_sc[:].rearrange("p a t -> p (a t)").bitcast(I32), 0)
        for t in w4_sc:
            nc.vector.memset(t[:].rearrange("p a t -> p (a t)").bitcast(I32), 0)
        nc.vector.memset(tab2_sc[:].bitcast(I32), 0)
        nc.gpsimd.memset(rows[:], 0.0)
        make_identity(nc, ident[:])

        idx = load_list(offs, "idx")
        idx3 = load_list(offs3, "idx3")
        idx2 = load_list(offs2, "idx2")
        p2 = load_list(pos2, "p2")
        p1 = load_list(pos1, "p1")

        w1_raw = {}
        w4_t = {}
        res_t = {}
        page_t = {}

        def load_w1(c0, passes):
            if c0 not in w1_raw:
                t = ring2.tile([P, KA, 4, 2 * P], F32, name="w1raw", tag="w1raw")
                for i in range(2):
                    w1_raw[c0 + i] = (t, i)
            for a in passes:
                nc.sync.dma_start(
                    w1_raw[c0][0][:, a, :, :],
                    w1[512 * a : 512 * (a + 1), c0 * P : (c0 + 2) * P].rearrange("(p j) c -> p j c", j=4),
                )

        def load_w4(c0, c1):
            t = keep.tile([P, KA, 2 * P * (c1 - c0)], U8, name=f"w4_{c0}", align_bytes=64)
            nc.sync.dma_start(
                t[:].bitcast(I32),
                w4_words[:, :, 2 * P * c0 : 2 * P * c1].rearrange("a p b -> p a b").bitcast(I32),
            )
            for c in range(c0, c1):
                w4_t[c] = (t, c - c0)

        def load_w4_scales(t, r0, r1):
            for q in range(4):
                nc.sync.dma_start(
                    t[32 * q : 32 * q + 4, :, :].bitcast(I32),
                    w4_scales[:, 4 * q : 4 * q + 4, r0:r1].rearrange("a r t -> r a t").bitcast(I32),
                )

        def load_res(c):
            t = keep.tile([P, S], F32, name=f"res{c}", tag=f"res{c}")
            nc.sync.dma_start(t[:], res[c * P : (c + 1) * P, :])
            res_t[c] = t

        def load_page(c):
            t = keep.tile([P, T2], F32, name=f"page{c}")
            nc.sync.dma_start(t[:], page0[c * P : (c + 1) * P, :])
            page_t[c] = t

        tabw = [load_words(tab_words, 0, "tabw0")]
        load_w4(*W4_PARTS[0])
        load_w1(0, [0])
        for q in range(4):
            nc.sync.dma_start(
                tab_sc[32 * q : 32 * q + 4, :, :].bitcast(I32),
                tab_scales[:, 4 * q : 4 * q + 4, :].rearrange("a r t -> r a t").bitcast(I32),
            )
        for a in range(1, KA):
            tabw.append(load_words(tab_words, a, f"tabw{a}"))
        nc.sync.dma_start(rows[0:TILES, :], b1.rearrange("(c p) -> c p", p=P))
        nc.sync.dma_start(rows[TILES : 2 * TILES, :], gain.rearrange("(c p) -> c p", p=P))
        load_w4_scales(w4_sc[0], 0, 2 * P)
        load_w1(0, range(1, KA))
        load_page(0)
        wgs_t = late.tile([P, S], F32, name="wgs_t", offset=2048, align_bytes=64)
        nc.sync.dma_start(wgs_t[:], wgs)
        load_res(0)
        load_w1(2, range(KA))
        load_w4_scales(w4_sc[1], 2 * P, H)
        load_w4(*W4_PARTS[1])
        for c in range(1, TILES):
            if c % 2 == 0 and c + 2 < TILES:
                load_w1(c + 2, range(KA))
            if c == 2:
                load_w4(*W4_PARTS[2])
            load_page(c)
            load_res(c)
        for q in range(4):
            nc.sync.dma_start(
                tab2_sc[32 * q : 32 * q + 4 * HA, :].bitcast(I32),
                tab2_scales[:, 4 * q : 4 * q + 4, :].bitcast(I32),
            )
        tab2w = [load_words(tab2_words, a, f"tab2w{a}") for a in range(HA)]
        rel_t = []
        for m in range(S2 // P):
            t = ends.tile([P, NP], F32, name=f"rel{m}", offset=4 * NP * m)
            nc.sync.dma_start(t[:], rel[m * P : (m + 1) * P, :])
            rel_t.append(t)

        bg_ps = psum.tile([P, BANK], F32, name="bg_ps", tag="t2")
        nc.tensor.transpose(bg_ps[:, 0:P], rows[:], ident[:])

        def bias_at(c):
            return ((c + 1) % 2) * 2432 + 2048 + 64 * ((c + 1) // 2)

        bias = []
        for c in range(TILES):
            t = held.tile([P, 1], F32, name=f"bias{c}", offset=bias_at(c), align_bytes=64)
            nc.scalar.copy(t[:], bg_ps[:, c : c + 1])
            bias.append(t)
        gains = keep.tile([P, TILES], F32, name="gains")
        nc.scalar.copy(gains[:], bg_ps[:, TILES : 2 * TILES])

        v_w = keep.tile([P, KA, S], I32, name="v_w", align_bytes=64)
        v_s = keep.tile([P, KA, S], U8, name="v_s", align_bytes=64)
        for a in range(KA):
            nc.vector.tensor_copy(v_w[:, a, :].bitcast(U32), tabw[a][:].bitcast(U32).indirect(idx[:]))
            nc.vector.tensor_copy(v_s[:, a, :], tab_sc[:, a, :].indirect(idx[:]))

        grouped = {}
        codes = {}
        bent = {}
        y_ps = {}
        summed = {}
        bounded = {}
        turned = {}
        pg = {}

        def round_w1(c):
            raw, i = w1_raw[c]
            g = ring2.tile([P, KA, P, 4], BF16, name="w1g", tag="w1g", align_bytes=64)
            for a in range(KA):
                nc.scalar.copy(
                    g[:, a, :, :].rearrange("p (g i) j -> p g j i", i=4),
                    raw[:, a, :, i * P : (i + 1) * P].rearrange("p j (g i) -> p g j i", i=4),
                )
            grouped[c] = g

        def quantise_w1(c, a0, a1):
            if a0 == 0:
                w1_w = held.tile([P, KA, P], I32, name=f"w1_w{c}", offset=bias_at(c - 1) + 64 - 1536, align_bytes=64)
                w1_s = ring2.tile([P, KA, P], U8, name="w1_s", tag="w1_s", align_bytes=64)
                codes[c] = (w1_w, w1_s)
            w1_w, w1_s = codes[c]
            nc.vector.quantize_mx(
                out=w1_w[:, a0:a1, :].rearrange("p a c -> p (a c)").bitcast(FP8X4),
                scales=w1_s[:, a0:a1, :].rearrange("p a c -> p (a c)"),
                in_=grouped[c][:, a0:a1, :, :].rearrange("p a c j -> p (a c j)"),
            )

        def product_w4(c):
            y = psum1.tile([P, S], F32, name="y", tag=f"p{c % 2}")
            w4, ci = w4_t[c]
            sc, si = (w4_sc[0], c) if c < 2 else (w4_sc[1], c - 2)
            for a in range(KA):
                nc.tensor.matmul_mx(
                    out=y[:], lhsT=w4[:, a, 2 * P * ci : 2 * P * (ci + 1)].bitcast(FP4X4),
                    lhsT_scale=sc[:, a, si * P : (si + 1) * P],
                    rhs=v_w[:, a, :].bitcast(FP8X4), rhs_scale=v_s[:, a, :],
                    start=(a == 0), stop=(a == KA - 1),
                )
            y_ps[c] = y

        def product_w1(c):
            w1_w, w1_s = codes[c]
            z = psum1.tile([P, S], F32, name="z", tag="z")
            for a in range(KA):
                nc.tensor.matmul_mx(
                    out=z[:], lhsT=w1_w[:, a, :].bitcast(FP8X4), lhsT_scale=w1_s[:, a, :],
                    rhs=v_w[:, a, :].bitcast(FP8X4), rhs_scale=v_s[:, a, :],
                    start=(a == 0), stop=(a == KA - 1),
                )
            t = ring2.tile([P, S], F32, name="bent", tag="bent")
            nc.scalar.activation(t[:], z[:], TANH, bias=bias[c][:])
            bent[c] = t

        def add_up(c):
            t = keep.tile([P, S], F32, name="summed", tag="summed")
            nc.vector.scalar_tensor_tensor(
                t[:], bent[c][:], gains[:, c : c + 1], y_ps[c][:], MULT, ADD
            )
            summed[c] = t

        def bound(c):
            h = held.tile([P, S], F32, name=f"h{c}", offset=(c % 2) * 2432, align_bytes=64)
            nc.vector.tensor_tensor(h[:], summed[c][:], res_t[c][:], MAX)
            bounded[c] = h

        def place(c):
            h = bounded[c]
            nc.vector.tensor_tensor(page_t[c][:].indirect(idx3[:]), h[:], wgs_t[:], MULT)

        def turn(c):
            a2, q = divmod(c, 4)
            for half in range(2):
                t1 = psum1.tile([P, 4, P], F32, name="t1", tag="z" if c == 0 else ("t1", f"p{(c + 1) % 2}")[half])
                if q == 0:
                    turned[a2, half] = keep.tile([P, 4, 2, 256], BF16, name=f"turned{a2}{half}", align_bytes=64)
                for b in range(4):
                    n0 = (4 * half + b) * P
                    nc.tensor.transpose(t1[:, b, :], page_t[c][:, n0 : n0 + P], ident[:])
                nc.scalar.copy(
                    turned[a2, half][:, :, :, 64 * q : 64 * (q + 1)].rearrange("p b u (m e) -> p b u m e", e=2),
                    t1[:].rearrange("p b (m u e) -> p b u m e", u=2, e=2),
                )

        def turn_back(a2, half):
            words = turned[a2, half][:].bitcast(F32)
            g = keep.tile([P, 4 * BANK], BF16, name="pg", tag=f"pg{a2}{half}", align_bytes=64)
            g_words = g[:].bitcast(F32).rearrange("p (b n u) -> p b n u", b=4, u=2)
            for pair in range(2):
                if a2 == 0:
                    t2 = psum1.tile([P, 2, 2, P], F32, name="t2", tag=("p0", "z")[pair])
                else:
                    t2 = psum.tile([P, 2, 2, P], F32, name="t2", tag="t2")
                for b in range(2):
                    for u in range(2):
                        nc.tensor.transpose(t2[:, b, u, :], words[:, 2 * pair + b, u, :], ident[:])
                nc.scalar.copy(g_words[:, 2 * pair : 2 * pair + 2, :, :], t2[:].rearrange("p b u n -> p b n u"))
            pg[a2, half] = g

        round_w1(0)
        round_w1(1)
        quantise_w1(0, 0, 2)
        quantise_w1(0, 2, 3)
        product_w4(0)
        product_w1(0)
        product_w4(1)
        for c in range(TILES):
            add_up(c)
            if c + 1 < TILES:
                quantise_w1(c + 1, 0, 2)
            bound(c)
            if c + 1 < TILES:
                quantise_w1(c + 1, 2, 3)
            place(c)
            if c + 2 < TILES:
                round_w1(c + 2)
            if c + 1 < TILES:
                product_w1(c + 1)
            if c >= 1:
                turn(c - 1)
            if c + 2 < TILES:
                product_w4(c + 2)
            if c == TILES - 2:
                for half in range(2):
                    turn_back(0, half)
        turn(TILES - 1)
        for half in range(2):
            turn_back(1, half)

        v2_s = late.tile([P, S2], U8, name="v2_s", offset=2560, align_bytes=64)
        page_s = late.tile([P, HA, T2], U8, name="page_s", offset=512, align_bytes=64)
        page_w = keep.tile([P, HA, T2], I32, name="page_w", align_bytes=64)
        v2_w = []

        def gather_v2(t, part):
            for a in range(HA):
                nc.vector.tensor_copy(
                    t[:, a, :].bitcast(U32), tab2w[a][:].bitcast(U32).indirect(idx2[:, 16 * part : 16 * (part + 1)])
                )
            v2_w.append(t)

        nc.vector.tensor_copy(v2_s[:], tab2_sc[:].indirect(idx2[:]))
        gather_v2(late.tile([P, HA, S2 // 2], I32, name="v2_lo", offset=3072, align_bytes=64), 0)
        for a in range(HA):
            for half in range(2):
                nc.vector.quantize_mx(
                    out=page_w[:, a, half * BANK : (half + 1) * BANK].bitcast(FP8X4),
                    scales=page_s[:, a, half * BANK : (half + 1) * BANK],
                    in_=pg[a, half][:],
                )
        gather_v2(keep.tile([P, HA, S2 // 2], I32, name="v2_hi", tag="pg11", align_bytes=64), 1)

        scores = {}
        lower = {}
        for m in range(S2 // P):
            e = keep.tile([P, T2], F32, name=f"e{m}")
            for half in range(2):
                if m % 2 == 0:
                    acc = psum.tile([P, BANK], F32, name="acc", tag="t2")
                else:
                    acc = psum1.tile([P, BANK], F32, name="acc", tag=("z", "p1")[half])
                order = range(HA) if m == 0 else reversed(range(HA))
                for i, a in enumerate(order):
                    nc.tensor.matmul_mx(
                        out=acc[:], lhsT=v2_w[m // 2][:, a, (m % 2) * P : (m % 2 + 1) * P].bitcast(FP8X4),
                        lhsT_scale=v2_s[4 * a : P, m * P : (m + 1) * P],
                        rhs=page_w[:, a, half * BANK : (half + 1) * BANK].bitcast(FP8X4),
                        rhs_scale=page_s[:, a, half * BANK : (half + 1) * BANK],
                        start=(i == 0), stop=(i == HA - 1),
                    )
                nc.scalar.copy(e[:, half * BANK : (half + 1) * BANK], acc[:])
            scores[m] = e
            t = keep.tile([P, NP], F32, name="lower", tag=f"res{m}")
            nc.vector.tensor_tensor(t[:], e[:].indirect(p2[:]), rel_t[m][:], MULT)
            lower[m] = t
        both = ends.tile([P, S2 // P, NP], F32, name="both", offset=0)
        for m in range(S2 // P):
            pieces = 2 if m == S2 // P - 1 else 1
            width = NP // pieces
            for j0 in range(0, NP, width):
                cols = slice(j0, j0 + width)
                picked = scores[m][:].indirect(p1[:, j0 // 16 : (j0 + width) // 16])
                nc.vector.tensor_tensor(both[:, m, cols], picked, lower[m][:, cols], ADD)
                nc.sync.dma_start(out[m * P : (m + 1) * P, cols], both[:, m, cols])
